import numpy as np
import ml_dtypes


def mxq(x, axis, fmt="e4m3"):
    dtype, down = {"e4m3": (ml_dtypes.float8_e4m3fn, 7), "e5m2": (ml_dtypes.float8_e5m2, 14)}[fmt]
    v = np.moveaxis(np.asarray(x, np.float32).astype(ml_dtypes.bfloat16).astype(np.float64), axis, -1)
    blocks = v.reshape(v.shape[:-1] + (-1, 32))
    amax = np.abs(blocks).max(-1, keepdims=True)
    byte = np.maximum(np.where(amax > 0, np.frexp(amax)[1] - 1 + 127, 0) - down, 1)
    scale = np.exp2(byte - 127.0)
    codes = (blocks / scale).astype(np.float32).astype(dtype).astype(np.float64)
    return np.moveaxis((codes * scale).reshape(v.shape), -1, axis)


WIDE = False


def mx_kscale(k):
    if not WIDE:
        return np.ones(k)
    levels = np.array([10, -10, 5, -5, 0])
    if k % 512:
        return np.exp2(np.random.permutation(np.resize(levels, k // 32))).repeat(32)
    a = np.empty((k // 512, 16))
    for p in range(k // 512):
        a[p, :8] = np.random.permutation(np.resize(levels, 8))
        for g in range(8):
            far = levels[np.abs(levels - a[p, g]) >= 10]
            a[p, g + 8] = far[np.random.randint(len(far))]
    return np.exp2(a.ravel()).repeat(32)


def f64(x):
    return np.asarray(x).astype(np.float64)


def striped(idx):
    return np.tile(idx.reshape(-1, 16).T, (8, 1)).astype(np.uint16)


def unstriped(offs):
    return offs[:16].T.reshape(-1).astype(np.int64)


def pack_weight(w):
    k, n = w.shape
    w = f64(np.asarray(w, np.float32).astype(ml_dtypes.bfloat16)).reshape(k // 32, 32, n)
    amax = np.abs(w).max(1)
    byte = np.clip(np.where(amax > 0, np.frexp(amax)[1] - 1 + 127 - 7, 1), 1, 254)
    scaled = (w * np.exp2(127.0 - byte)[:, None, :]).reshape(k, n).astype(np.float32)
    words = np.ascontiguousarray(scaled.reshape(k // 512, 128, 4, n).transpose(0, 1, 3, 2)).astype(ml_dtypes.float8_e4m3fn).view(np.uint8)
    return words, np.ascontiguousarray(byte.astype(np.uint8).reshape(k // 512, 16, n))


def unpack_weight(words, scales):
    g, p, n, _ = words.shape
    vals = np.ascontiguousarray(words).view(ml_dtypes.float8_e4m3fn).astype(np.float64) * np.repeat(np.exp2(scales.astype(np.float64) - 127.0), 8, axis=1)[..., None]
    return vals.transpose(0, 1, 3, 2).reshape(g * 512, n)


E2M1 = np.array([0.0, 0.5, 1.0, 1.5, 2.0, 3.0, 4.0, 6.0, -0.0, -0.5, -1.0, -1.5, -2.0, -3.0, -4.0, -6.0])


def pack_fp4(w):
    k, n = w.shape
    w = f64(np.asarray(w, np.float32).astype(ml_dtypes.bfloat16)).reshape(k // 32, 32, n)
    amax = np.abs(w).max(1)
    mant, ex = np.frexp(amax / 6.0)
    byte = np.clip(np.where(amax > 0, np.where(mant > 0.5, ex, ex - 1) + 127, 1), 1, 254)
    scaled = (w * np.exp2(127.0 - byte)[:, None, :]).reshape(k, n).astype(np.float32)
    c = np.ascontiguousarray(scaled.reshape(k // 512, 128, 4, n).transpose(0, 1, 3, 2)).astype(ml_dtypes.float4_e2m1fn).view(np.uint8) & 0xF
    words = (c[..., 0::2] | (c[..., 1::2] << 4)).reshape(k // 512, 128, 2 * n)
    return np.ascontiguousarray(words), np.ascontiguousarray(byte.astype(np.uint8).reshape(k // 512, 16, n))


def unpack_fp4(words, scales):
    g, _, n = scales.shape
    words = np.ascontiguousarray(words).reshape(g, 128, n, 2)
    nib = np.empty((g, 128, n, 4), np.uint8)
    nib[..., 0::2] = words & 0xF
    nib[..., 1::2] = words >> 4
    vals = E2M1[nib] * np.repeat(np.exp2(scales.astype(np.float64) - 127.0), 8, axis=1)[..., None]
    return vals.transpose(0, 1, 3, 2).reshape(g * 512, n)


def planes(y):
    n, m = y.shape
    v = y.astype(np.float32).astype(ml_dtypes.bfloat16).astype(np.float64).reshape(n // 32, 32, m)
    top = np.abs(v).max(1)
    byte = np.clip(np.where(top > 0, np.frexp(top)[1] - 1 + 127 - 7, 1), 1, 254)
    codes = (v * np.exp2(127.0 - byte)[:, None, :]).reshape(n, m).astype(np.float32).astype(ml_dtypes.float8_e4m3fn).view(np.uint8)
    words = codes.reshape(n // 512, 128, 4, m).transpose(0, 1, 3, 2)
    return np.ascontiguousarray(words), np.ascontiguousarray(byte.astype(np.uint8).reshape(n // 512, 16, m))


K, T, S, D, V, H, N = 512, 2048, 1024, 4, 512, 512, 512
P = 2 ** 7


def setup_inputs():
    n = np.random.standard_normal
    s = mx_kscale(K)[:, None]
    u = mx_kscale(H)
    near = np.random.permutation(S)
    packed_xT = pack_weight(n((K, T)) * s)
    packed_w2 = pack_fp4(n((H, N)) / np.sqrt(H) / u[:, None])
    return {
        "x_words": packed_xT[0],
        "x_scales": packed_xT[1],
        "w1": (n((K, H)) / np.sqrt(K) / s * u).astype(np.float32),
        "w2_words": packed_w2[0],
        "w2_scales": packed_w2[1],
        "gate": (np.tile(np.random.uniform(0.1, 0.6, (D, 1, V)), (1, P, 1))).astype(np.float32),
        "ref": (n((H, V)) * u[:, None]).astype(np.float32),
        "offs": striped(np.random.permutation(T)[:S]),
        "pos1": striped(near[:V]),
        "pos2": striped(near[V:]),
        "pos3": striped(np.random.permutation(S)[:V]),
        "pos4": striped(np.random.permutation(S)[:V]),
    }


def reference(x_words, x_scales, w1, w2_words, w2_scales, gate, ref, offs, pos1, pos2, pos3, pos4):
    xq = unpack_weight(x_words, x_scales)[:, unstriped(offs)]
    f = mxq(f64(w1), 0, "e4m3").T @ xq
    e = f64(ref) - (f[:, unstriped(pos1)] * f64(gate)[0, :1] + f[:, unstriped(pos2)] * f64(gate)[1, :1] + f[:, unstriped(pos3)] * f64(gate)[2, :1] + f[:, unstriped(pos4)] * f64(gate)[3, :1])
    z = np.abs(e)
    out_0 = unpack_fp4(w2_words, w2_scales).T @ mxq(z, 0, "e4m3")
    return (out_0,) + planes(out_0)

@@ -1,0 +1,270 @@
+from contextlib import ExitStack
+
+import concourse.mybir as mybir
+from concourse.masks import make_identity
+
+K, T, S, D, V, H, N = 512, 2048, 1024, 4, 512, 512, 512
+FLOPS = 2 * K * H * S + 2 * H * N * V
+
+F32 = mybir.dt.float32
+BF16 = mybir.dt.bfloat16
+I32 = mybir.dt.int32
+U32 = mybir.dt.uint32
+U16 = mybir.dt.uint16
+U8 = mybir.dt.uint8
+FP8X4 = mybir.dt.float8_e4m3fn_x4
+FP4X4 = mybir.dt.float4_e2m1fn_x4
+ACT = mybir.ActivationFunctionType
+MULT = mybir.AluOpType.mult
+
+P = 128
+PACK = 4
+BANK = 512
+
+
+def tile_picked_zwarp_abs_po_kernel(
+    tc, x_words, x_scales, w1, w2_words, w2_scales, gate, ref, offs, pos1, pos2, pos3, pos4, out_0, out_1, out_2
+):
+    nc = tc.nc
+    with ExitStack() as ctx:
+        keep = ctx.enter_context(tc.tile_pool(name="keep", bufs=1))
+        terms = ctx.enter_context(tc.tile_pool(name="terms", bufs=8))
+        sums = ctx.enter_context(tc.psum_pool(name="sums", bufs=1))
+        ring = ctx.enter_context(tc.psum_pool(name="ring", bufs=4))
+
+        def sb(shape, dtype, name):
+            return keep.tile(shape, dtype, name=name, align_bytes=64)
+
+        xs = sb([P, T], U8, "xs")
+        nc.gpsimd.memset(xs[:].bitcast(I32), 0)
+        w2s = sb([P, N], U8, "w2s")
+        nc.vector.memset(w2s[:].bitcast(I32), 0)
+
+        picks = keep.tile([P, S // 16], U16, name="picks")
+        nc.sync.dma_start(picks[:], offs)
+        gcol = sb([P, D, PACK], F32, "gcol")
+        nc.sync.dma_start(gcol[:], gate[:, 0, :].rearrange("d (p j) -> p d j", j=PACK))
+        for q in range(4):
+            nc.sync.dma_start(xs[32 * q : 32 * q + 4, :].bitcast(I32), x_scales[0, 4 * q : 4 * q + 4, :].bitcast(I32))
+        w1_rows = w1.rearrange("(p j) c -> p j c", j=PACK)
+        w1_raw = [sb([P, PACK, P], F32, f"w1_raw{t}") for t in range(4)]
+
+        def load_w1(t):
+            nc.sync.dma_start(w1_raw[t][:], w1_rows[:, :, t * P : (t + 1) * P])
+
+        ref_rows = ref.rearrange("(t p) v -> p t v", p=P)
+        ref_sb = [sb([P, 4, V // 2], F32, f"ref{h}") for h in range(2)]
+
+        def load_ref(h):
+            nc.sync.dma_start(ref_sb[h][:], ref_rows[:, :, h * (V // 2) : (h + 1) * (V // 2)])
+
+        xw = sb([P, T], U32, "xw")
+        nc.sync.dma_start(xw[:].bitcast(I32), x_words[0].rearrange("p n r -> p (n r)").bitcast(I32))
+        pos = []
+        for d, src in enumerate((pos1, pos2, pos3, pos4)):
+            lst = keep.tile([P, V // 16], U16, name=f"pos{d}")
+            nc.sync.dma_start(lst[:], src)
+            pos.append(lst)
+        for t in range(4):
+            load_w1(t)
+        w2w = sb([P, 2 * N], U8, "w2w")
+        nc.sync.dma_start(w2w[:].bitcast(I32), w2_words[0].bitcast(I32))
+        load_ref(0)
+        for q in range(4):
+            nc.sync.dma_start(w2s[32 * q : 32 * q + 4, :].bitcast(I32), w2_scales[0, 4 * q : 4 * q + 4, :].bitcast(I32))
+        load_ref(1)
+
+        ident = sb([P, P], F32, "ident")
+        make_identity(nc, ident[:])
+
+        w1_codes = [sb([P, P], U32, f"w1_codes{h}") for h in range(4)]
+        w1_scales = [sb([P, P], U8, f"w1_scales{h}") for h in range(4)]
+        w1_bf = [sb([P, P, PACK], BF16, f"w1_bf{h}") for h in range(4)]
+
+        def round_w1(h):
+            nc.scalar.activation(w1_bf[h][:], w1_raw[h][:].rearrange("p j c -> p c j"), ACT.Copy)
+
+        def quantise_w1(h):
+            nc.vector.quantize_mx(
+                out=w1_codes[h][:].bitcast(FP8X4), scales=w1_scales[h][:], in_=w1_bf[h][:].rearrange("p c j -> p (c j)")
+            )
+
+        gneg = sb([P, D, V], F32, "gneg")
+        for d in range(D):
+            spread = sums.tile([P, PACK, P], F32, name=f"spread{d}", tag=f"sum{d}")
+            for j in range(PACK):
+                nc.tensor.transpose(spread[:, j, :], gcol[:, d, j : j + 1].to_broadcast([P, P]), ident[:])
+            nc.scalar.activation(
+                gneg[:, d, :].rearrange("m (p j) -> m p j", j=PACK), spread[:].rearrange("m j p -> m p j"), ACT.Copy, scale=-1.0
+            )
+
+        xg_s = [sb([P, BANK], U8, f"xg_s{h}") for h in range(2)]
+        xg_w = [sb([P, BANK], U32, f"xg_w{h}") for h in range(2)]
+        f = [sb([P, S], F32, f"f{t}") for t in range(4)]
+
+        def first(t, h):
+            acc = ring.tile([P, BANK], F32, name="acc", tag="ring")
+            nc.tensor.matmul_mx(
+                out=acc[:],
+                lhsT=w1_codes[t][:].bitcast(FP8X4),
+                lhsT_scale=w1_scales[t][:],
+                rhs=xg_w[h][:].bitcast(FP8X4),
+                rhs_scale=xg_s[h][:],
+                start=True,
+                stop=True,
+            )
+            if (t, h) == (0, 1):
+                nc.vector.tensor_copy(f[t][:, h * BANK : (h + 1) * BANK], acc[:])
+            else:
+                nc.scalar.copy(f[t][:, h * BANK : (h + 1) * BANK], acc[:])
+
+        w2w_dealt = sb([P, 2 * N], U8, "w2w_dealt")
+        w2s_dealt = sb([P, N], U8, "w2s_dealt")
+
+        def deal_words():
+            nc.vector.tensor_copy(
+                w2w_dealt[:].rearrange("p (t m e) -> p t m e", t=PACK, e=2), w2w[:].rearrange("p (m t e) -> p t m e", t=PACK, e=2)
+            )
+
+        def deal_scales():
+            nc.vector.tensor_copy(w2s_dealt[:].rearrange("p (t m) -> p t m", t=PACK), w2s[:].rearrange("p (m t) -> p t m", t=PACK))
+
+        for h in range(2):
+            nc.vector.tensor_copy(xg_s[h][:], xs[:].indirect(picks[:, 32 * h : 32 * (h + 1)]))
+        nc.vector.tensor_copy(xg_w[0][:], xw[:].indirect(picks[:, 0:32]))
+        round_w1(0)
+        quantise_w1(0)
+        nc.vector.tensor_copy(xg_w[1][:], xw[:].indirect(picks[:, 32:64]))
+        round_w1(1)
+        quantise_w1(1)
+        first(0, 0)
+        first(0, 1)
+        round_w1(2)
+        quantise_w1(2)
+        first(1, 0)
+        first(1, 1)
+        round_w1(3)
+        quantise_w1(3)
+        for t in (2, 3):
+            first(t, 0)
+            first(t, 1)
+
+        e_t = [sums.tile([P, H], F32, name=f"e{b}", tag=f"sum{b}") for b in range(4)]
+
+        def add_turned(b, t, block, start, stop):
+            nc.tensor.matmul(e_t[b][:, t * P : (t + 1) * P], lhsT=block, rhs=ident[:], start=start, stop=stop, is_transpose=True)
+
+        def open_sums(b):
+            for t in range(4):
+                add_turned(b, t, ref_sb[b // 2][:, t, (b % 2) * P : (b % 2 + 1) * P], t == 0, False)
+
+        W = V // 2
+        late = {}
+
+        def fetch(half, t, fused):
+            ls = slice(half * (W // 16), (half + 1) * (W // 16))
+            late[half, t] = terms.tile([P, D - fused, W], F32, name="late", tag="late", align_bytes=64, bufs=8)
+            for d in range(fused, D):
+                nc.scalar.activation(late[half, t][:, d - fused, :], f[t][:].indirect(pos[d][:, ls]), ACT.Copy)
+
+        def weigh(half, t, fused):
+            vs = slice(half * W, (half + 1) * W)
+            ls = slice(half * (W // 16), (half + 1) * (W // 16))
+            term = [terms.tile([P, W], F32, name=f"term{d}", tag=f"term{d}", align_bytes=64) for d in range(fused)]
+            for d in range(fused):
+                nc.vector.tensor_tensor(term[d][:], f[t][:].indirect(pos[d][:, ls]), gneg[:, d, vs], MULT)
+            nc.vector.tensor_tensor(late[half, t][:], late[half, t][:], gneg[:, fused:D, vs], MULT)
+            for d in range(D):
+                for s in range(2):
+                    cols = slice(s * P, (s + 1) * P)
+                    block = term[d][:, cols] if d < fused else late[half, t][:, d - fused, cols]
+                    add_turned(2 * half + s, t, block, False, t == 3 and d == D - 1)
+
+        def corners(half, t, fused):
+            fetch(half, t, fused)
+            weigh(half, t, fused)
+
+        out_codes = sb([P, V], U32, "out_codes")
+        out_scales = sb([P, V], U8, "out_scales")
+        out_rows = out_0.rearrange("(p t) v -> p t v", t=PACK)
+        out_words = out_1[0].rearrange("p n r -> p (n r)").bitcast(I32)
+        z = [sb([P, H], BF16, f"z{b}") for b in range(4)]
+        y = [sb([P, PACK, P], F32, f"y{b}") for b in range(4)]
+
+        z_t = [sb([P, H], BF16, f"z_t{b}") for b in range(4)]
+
+        def magnitude(b):
+            nc.scalar.activation(
+                z_t[b][:].rearrange("v (u q e) -> v u q e", u=2, e=2), e_t[b][:].rearrange("v (q u e) -> v u q e", u=2, e=2), ACT.Abs
+            )
+
+        def turn_back(b):
+            turned = ring.tile([P, 2, P], F32, name="turned", tag="ring")
+            for u in range(2):
+                nc.tensor.transpose(turned[:, u, :], z_t[b][:].bitcast(F32)[:, u * P : (u + 1) * P], ident[:])
+            words = z[b][:].bitcast(F32).rearrange("p (v u) -> p v u", u=2)
+            if b < 2:
+                nc.scalar.copy(words, turned[:].rearrange("p u v -> p v u"))
+            else:
+                nc.vector.tensor_copy(words, turned[:].rearrange("p u v -> p v u"))
+
+        def second(b):
+            z_codes = sb([P, P], U32, f"z_codes{b}")
+            z_scales = sb([P, P], U8, f"z_scales{b}")
+            nc.vector.quantize_mx(out=z_codes[:].bitcast(FP8X4), scales=z_scales[:], in_=z[b][:])
+            acc = ring.tile([P, PACK, P], F32, name="acc2", tag="ring")
+            for t in range(PACK):
+                nc.tensor.matmul_mx(
+                    out=acc[:, t, :],
+                    lhsT=w2w_dealt[:, 2 * P * t : 2 * P * (t + 1)].bitcast(FP4X4),
+                    lhsT_scale=w2s_dealt[:, P * t : P * (t + 1)],
+                    rhs=z_codes[:].bitcast(FP8X4),
+                    rhs_scale=z_scales[:],
+                    start=True,
+                    stop=True,
+                )
+            nc.scalar.copy(y[b][:], acc[:])
+            nc.sync.dma_start(out_rows[:, :, b * P : (b + 1) * P], y[b][:])
+
+        def planes(b):
+            vs = slice(b * P, (b + 1) * P)
+            y_bf = sb([P, P, PACK], BF16, f"y_bf{b}")
+            nc.vector.tensor_copy(y_bf[:], y[b][:].rearrange("p t v -> p v t"))
+            nc.vector.quantize_mx(
+                out=out_codes[:, vs].bitcast(FP8X4), scales=out_scales[:, vs], in_=y_bf[:].rearrange("p v t -> p (v t)")
+            )
+
+        deal_words()
+        open_sums(0)
+        open_sums(1)
+        corners(0, 0, 3)
+        corners(0, 1, 2)
+        deal_scales()
+        corners(0, 2, 2)
+        open_sums(2)
+        open_sums(3)
+        corners(0, 3, 2)
+        corners(1, 0, 2)
+        magnitude(0)
+        magnitude(1)
+        corners(1, 1, 2)
+        turn_back(0)
+        turn_back(1)
+        corners(1, 2, 2)
+        second(0)
+        second(1)
+        corners(1, 3, 2)
+        magnitude(2)
+        magnitude(3)
+        turn_back(2)
+        turn_back(3)
+        second(2)
+        second(3)
+        for half in range(2):
+            planes(2 * half)
+            planes(2 * half + 1)
+            vs = slice(half * W, (half + 1) * W)
+            nc.sync.dma_start(out_words[:, vs], out_codes[:, vs].bitcast(I32))
+        for q in range(4):
+            queue = nc.sync if q < 2 else nc.scalar
+            queue.dma_start(out_2[0, 4 * q : 4 * q + 4, :].bitcast(I32), out_scales[32 * q : 32 * q + 4, :].bitcast(I32))

@@ -28,7 +28,6 @@ def tile_picked_zwarp_abs_po_kernel(
     nc = tc.nc
     with ExitStack() as ctx:
         keep = ctx.enter_context(tc.tile_pool(name="keep", bufs=1))
-        terms = ctx.enter_context(tc.tile_pool(name="terms", bufs=8))
         sums = ctx.enter_context(tc.psum_pool(name="sums", bufs=1))
         ring = ctx.enter_context(tc.psum_pool(name="ring", bufs=4))
 
@@ -42,8 +41,8 @@ def tile_picked_zwarp_abs_po_kernel(
 
         picks = keep.tile([P, S // 16], U16, name="picks")
         nc.sync.dma_start(picks[:], offs)
-        gcol = sb([P, D, PACK], F32, "gcol")
-        nc.sync.dma_start(gcol[:], gate[:, 0, :].rearrange("d (p j) -> p d j", j=PACK))
+        gcol = sb([P, 16], F32, "gcol")
+        nc.sync.dma_start(gcol[:], gate.rearrange("d r (c j) -> (d r c) j", j=16)[0 : D * P * 32 : P + 1, :])
         for q in range(4):
             nc.sync.dma_start(xs[32 * q : 32 * q + 4, :].bitcast(I32), x_scales[0, 4 * q : 4 * q + 4, :].bitcast(I32))
         w1_rows = w1.rearrange("(p j) c -> p j c", j=PACK)
@@ -59,20 +58,23 @@ def tile_picked_zwarp_abs_po_kernel(
             nc.sync.dma_start(ref_sb[h][:], ref_rows[:, :, h * (V // 2) : (h + 1) * (V // 2)])
 
         xw = sb([P, T], U32, "xw")
-        nc.sync.dma_start(xw[:].bitcast(I32), x_words[0].rearrange("p n r -> p (n r)").bitcast(I32))
+        x_rows = x_words[0].rearrange("p n r -> p (n r)").bitcast(I32)
+        for h in range(2):
+            cols = slice(h * (T // 2), (h + 1) * (T // 2))
+            nc.sync.dma_start(xw[:, cols].bitcast(I32), x_rows[:, cols])
+        for t in range(4):
+            load_w1(t)
         pos = []
         for d, src in enumerate((pos1, pos2, pos3, pos4)):
             lst = keep.tile([P, V // 16], U16, name=f"pos{d}")
             nc.sync.dma_start(lst[:], src)
             pos.append(lst)
-        for t in range(4):
-            load_w1(t)
+        load_ref(0)
+        load_ref(1)
         w2w = sb([P, 2 * N], U8, "w2w")
         nc.sync.dma_start(w2w[:].bitcast(I32), w2_words[0].bitcast(I32))
-        load_ref(0)
         for q in range(4):
             nc.sync.dma_start(w2s[32 * q : 32 * q + 4, :].bitcast(I32), w2_scales[0, 4 * q : 4 * q + 4, :].bitcast(I32))
-        load_ref(1)
 
         ident = sb([P, P], F32, "ident")
         make_identity(nc, ident[:])
@@ -90,20 +92,22 @@ def tile_picked_zwarp_abs_po_kernel(
             )
 
         gneg = sb([P, D, V], F32, "gneg")
-        for d in range(D):
-            spread = sums.tile([P, PACK, P], F32, name=f"spread{d}", tag=f"sum{d}")
-            for j in range(PACK):
-                nc.tensor.transpose(spread[:, j, :], gcol[:, d, j : j + 1].to_broadcast([P, P]), ident[:])
-            nc.scalar.activation(
-                gneg[:, d, :].rearrange("m (p j) -> m p j", j=PACK), spread[:].rearrange("m j p -> m p j"), ACT.Copy, scale=-1.0
-            )
+        gneg_by_run = gneg[:].rearrange("m d (c j) -> m (d c) j", j=16)
+        for k in range(4):
+            spread = sums.tile([P, 4, P], F32, name=f"spread{k}", tag=f"sum{k}")
+            for j in range(4):
+                nc.tensor.transpose(spread[:, j, :], gcol[:, 4 * k + j : 4 * k + j + 1].to_broadcast([P, P]), ident[:])
+            nc.scalar.activation(gneg_by_run[:, :, 4 * k : 4 * k + 4], spread[:].rearrange("m j p -> m p j"), ACT.Copy, scale=-1.0)
 
         xg_s = [sb([P, BANK], U8, f"xg_s{h}") for h in range(2)]
         xg_w = [sb([P, BANK], U32, f"xg_w{h}") for h in range(2)]
         f = [sb([P, S], F32, f"f{t}") for t in range(4)]
 
         def first(t, h):
-            acc = ring.tile([P, BANK], F32, name="acc", tag="ring")
+            if t < 2:
+                acc = sums.tile([P, BANK], F32, name=f"acc{t}_{h}", tag=f"sum{2 * t + h}")
+            else:
+                acc = ring.tile([P, BANK], F32, name="acc", tag="ring")
             nc.tensor.matmul_mx(
                 out=acc[:],
                 lhsT=w1_codes[t][:].bitcast(FP8X4),
@@ -159,30 +163,31 @@ def tile_picked_zwarp_abs_po_kernel(
                 add_turned(b, t, ref_sb[b // 2][:, t, (b % 2) * P : (b % 2 + 1) * P], t == 0, False)
 
         W = V // 2
-        late = {}
+        on_vector = [(t, d) for t in range(4) for d in range(D) if d < 2 or (d == 2 and t < 0)]
+        on_scalar = {d: [t for t in range(4) if (t, d) not in on_vector] for d in (2, 3)}
+        late = {(half, d): sb([P, len(on_scalar[d]), W], F32, f"late{half}_{d}") for half in range(2) for d in (2, 3)}
 
-        def fetch(half, t, fused):
+        def fused(t, d):
+            term = sb([P, V], F32, f"term{t}_{d}")
+            nc.vector.tensor_tensor(term[:], f[t][:].indirect(pos[d][:]), gneg[:, d, :], MULT)
+            for b in range(4):
+                add_turned(b, t, term[:, b * P : (b + 1) * P], False, False)
+
+        def fetch(half):
             ls = slice(half * (W // 16), (half + 1) * (W // 16))
-            late[half, t] = terms.tile([P, D - fused, W], F32, name="late", tag="late", align_bytes=64, bufs=8)
-            for d in range(fused, D):
-                nc.scalar.activation(late[half, t][:, d - fused, :], f[t][:].indirect(pos[d][:, ls]), ACT.Copy)
+            for t in range(4):
+                for d in (2, 3):
+                    if t in on_scalar[d]:
+                        nc.scalar.activation(late[half, d][:, on_scalar[d].index(t), :], f[t][:].indirect(pos[d][:, ls]), ACT.Copy)
 
-        def weigh(half, t, fused):
-            vs = slice(half * W, (half + 1) * W)
-            ls = slice(half * (W // 16), (half + 1) * (W // 16))
-            term = [terms.tile([P, W], F32, name=f"term{d}", tag=f"term{d}", align_bytes=64) for d in range(fused)]
-            for d in range(fused):
-                nc.vector.tensor_tensor(term[d][:], f[t][:].indirect(pos[d][:, ls]), gneg[:, d, vs], MULT)
-            nc.vector.tensor_tensor(late[half, t][:], late[half, t][:], gneg[:, fused:D, vs], MULT)
-            for d in range(D):
-                for s in range(2):
-                    cols = slice(s * P, (s + 1) * P)
-                    block = term[d][:, cols] if d < fused else late[half, t][:, d - fused, cols]
-                    add_turned(2 * half + s, t, block, False, t == 3 and d == D - 1)
-
-        def corners(half, t, fused):
-            fetch(half, t, fused)
-            weigh(half, t, fused)
+        def weigh(b):
+            cols = slice((b % 2) * P, (b % 2 + 1) * P)
+            for d in (2, 3):
+                rows = late[b // 2, d][:, :, cols]
+                n = len(on_scalar[d])
+                nc.vector.tensor_tensor(rows, rows, gneg[:, d : d + 1, b * P : (b + 1) * P].to_broadcast([P, n, P]), MULT)
+                for k, t in enumerate(on_scalar[d]):
+                    add_turned(b, t, late[b // 2, d][:, k, cols], False, d == 3 and t == 3)
 
         out_codes = sb([P, V], U32, "out_codes")
         out_scales = sb([P, V], U8, "out_scales")
@@ -212,7 +217,7 @@ def tile_picked_zwarp_abs_po_kernel(
             z_codes = sb([P, P], U32, f"z_codes{b}")
             z_scales = sb([P, P], U8, f"z_scales{b}")
             nc.vector.quantize_mx(out=z_codes[:].bitcast(FP8X4), scales=z_scales[:], in_=z[b][:])
-            acc = ring.tile([P, PACK, P], F32, name="acc2", tag="ring")
+            acc = sums.tile([P, PACK, P], F32, name=f"acc2_{b}", tag=f"sum{b}")
             for t in range(PACK):
                 nc.tensor.matmul_mx(
                     out=acc[:, t, :],
@@ -235,31 +240,20 @@ def tile_picked_zwarp_abs_po_kernel(
             )
 
         deal_words()
-        open_sums(0)
-        open_sums(1)
-        corners(0, 0, 3)
-        corners(0, 1, 2)
+        for b in range(4):
+            open_sums(b)
+        for t, d in on_vector:
+            fused(t, d)
         deal_scales()
-        corners(0, 2, 2)
-        open_sums(2)
-        open_sums(3)
-        corners(0, 3, 2)
-        corners(1, 0, 2)
-        magnitude(0)
-        magnitude(1)
-        corners(1, 1, 2)
-        turn_back(0)
-        turn_back(1)
-        corners(1, 2, 2)
-        second(0)
-        second(1)
-        corners(1, 3, 2)
-        magnitude(2)
-        magnitude(3)
-        turn_back(2)
-        turn_back(3)
-        second(2)
-        second(3)
+        for half in range(2):
+            fetch(half)
+        for b in range(4):
+            weigh(b)
+        for b in range(4):
+            magnitude(b)
+            turn_back(b)
+        for b in range(4):
+            second(b)
         for half in range(2):
             planes(2 * half)
             planes(2 * half + 1)

@@ -1,7 +1,6 @@
 from contextlib import ExitStack
 
 import concourse.mybir as mybir
-from concourse.masks import make_identity
 
 K, T, S, D, V, H, N = 512, 2048, 1024, 4, 512, 512, 512
 FLOPS = 2 * K * H * S + 2 * H * N * V
@@ -16,6 +15,7 @@ FP8X4 = mybir.dt.float8_e4m3fn_x4
 FP4X4 = mybir.dt.float4_e2m1fn_x4
 ACT = mybir.ActivationFunctionType
 MULT = mybir.AluOpType.mult
+ADD = mybir.AluOpType.add
 
 P = 128
 PACK = 4
@@ -36,8 +36,19 @@ def tile_picked_zwarp_abs_po_kernel(
 
         xs = sb([P, T], U8, "xs")
         nc.gpsimd.memset(xs[:].bitcast(I32), 0)
+        ones = sb([P, 32], F32, "ones")
+        nc.vector.memset(ones[:], 1.0)
+        ident = sb([P, P], F32, "ident")
+        nc.vector.memset(ident[:], 0.0)
+        column = sb([P, 32], F32, "column")
+        nc.vector.tensor_tensor_scan(column[:], ones[:], ones[:], 0.0, MULT, ADD)
         w2s = sb([P, N], U8, "w2s")
         nc.vector.memset(w2s[:].bitcast(I32), 0)
+        row = sb([P, 32], F32, "row")
+        nc.vector.transpose(row[:], column[:])
+        for q in range(4):
+            part = slice(32 * q, 32 * (q + 1))
+            nc.vector.tensor_tensor(ident[part, part], column[part, :], row[part, :], mybir.AluOpType.is_equal)
 
         picks = keep.tile([P, S // 16], U16, name="picks")
         nc.sync.dma_start(picks[:], offs)
@@ -75,9 +86,6 @@ def tile_picked_zwarp_abs_po_kernel(
         nc.sync.dma_start(w2w[:].bitcast(I32), w2_words[0].bitcast(I32))
         for q in range(4):
             nc.sync.dma_start(w2s[32 * q : 32 * q + 4, :].bitcast(I32), w2_scales[0, 4 * q : 4 * q + 4, :].bitcast(I32))
-
-        ident = sb([P, P], F32, "ident")
-        make_identity(nc, ident[:])
 
         w1_codes = [sb([P, P], U32, f"w1_codes{h}") for h in range(4)]
         w1_scales = [sb([P, P], U8, f"w1_scales{h}") for h in range(4)]
@@ -122,17 +130,6 @@ def tile_picked_zwarp_abs_po_kernel(
             else:
                 nc.scalar.copy(f[t][:, h * BANK : (h + 1) * BANK], acc[:])
 
-        w2w_dealt = sb([P, 2 * N], U8, "w2w_dealt")
-        w2s_dealt = sb([P, N], U8, "w2s_dealt")
-
-        def deal_words():
-            nc.vector.tensor_copy(
-                w2w_dealt[:].rearrange("p (t m e) -> p t m e", t=PACK, e=2), w2w[:].rearrange("p (m t e) -> p t m e", t=PACK, e=2)
-            )
-
-        def deal_scales():
-            nc.vector.tensor_copy(w2s_dealt[:].rearrange("p (t m) -> p t m", t=PACK), w2s[:].rearrange("p (m t) -> p t m", t=PACK))
-
         for h in range(2):
             nc.vector.tensor_copy(xg_s[h][:], xs[:].indirect(picks[:, 32 * h : 32 * (h + 1)]))
         nc.vector.tensor_copy(xg_w[0][:], xw[:].indirect(picks[:, 0:32]))
@@ -160,34 +157,39 @@ def tile_picked_zwarp_abs_po_kernel(
 
         def open_sums(b):
             for t in range(4):
-                add_turned(b, t, ref_sb[b // 2][:, t, (b % 2) * P : (b % 2 + 1) * P], t == 0, False)
+                add_turned(b, t, ref_sb[b // 2][:, t, (b % 2) * P : (b % 2 + 1) * P], False, False)
 
         W = V // 2
-        on_vector = [(t, d) for t in range(4) for d in range(D) if d < 2 or (d == 2 and t < 0)]
-        on_scalar = {d: [t for t in range(4) if (t, d) not in on_vector] for d in (2, 3)}
-        late = {(half, d): sb([P, len(on_scalar[d]), W], F32, f"late{half}_{d}") for half in range(2) for d in (2, 3)}
+        rows_on_scalar = {2: list(range(1, 4)), 3: list(range(4))}
+        late = {d: sb([P, len(rows_on_scalar[d]), V], F32, f"late{d}") for d in (2, 3)}
 
         def fused(t, d):
             term = sb([P, V], F32, f"term{t}_{d}")
             nc.vector.tensor_tensor(term[:], f[t][:].indirect(pos[d][:]), gneg[:, d, :], MULT)
             for b in range(4):
-                add_turned(b, t, term[:, b * P : (b + 1) * P], False, False)
+                add_turned(b, t, term[:, b * P : (b + 1) * P], (t, d) == (0, 0), False)
 
-        def fetch(half):
-            ls = slice(half * (W // 16), (half + 1) * (W // 16))
-            for t in range(4):
-                for d in (2, 3):
-                    if t in on_scalar[d]:
-                        nc.scalar.activation(late[half, d][:, on_scalar[d].index(t), :], f[t][:].indirect(pos[d][:, ls]), ACT.Copy)
+        def fetch(d):
+            for k, t in enumerate(rows_on_scalar[d]):
+                nc.scalar.activation(late[d][:, k, :], f[t][:].indirect(pos[d][:]), ACT.Copy)
 
-        def weigh(b):
-            cols = slice((b % 2) * P, (b % 2 + 1) * P)
-            for d in (2, 3):
-                rows = late[b // 2, d][:, :, cols]
-                n = len(on_scalar[d])
-                nc.vector.tensor_tensor(rows, rows, gneg[:, d : d + 1, b * P : (b + 1) * P].to_broadcast([P, n, P]), MULT)
-                for k, t in enumerate(on_scalar[d]):
-                    add_turned(b, t, late[b // 2, d][:, k, cols], False, d == 3 and t == 3)
+        def weigh(d, b0, blocks):
+            vs = slice(b0 * P, (b0 + blocks) * P)
+            rows = late[d][:, :, vs]
+            weights = gneg[:, d : d + 1, vs].to_broadcast([P, len(rows_on_scalar[d]), blocks * P])
+            nc.vector.tensor_tensor(rows, rows, weights, MULT)
+            for b in range(b0, b0 + blocks):
+                for k, t in enumerate(rows_on_scalar[d]):
+                    add_turned(b, t, late[d][:, k, b * P : (b + 1) * P], False, d == 3 and t == 3)
+
+        w2w_dealt = keep.tile([P, 2 * N], U8, name="w2w_dealt", tag="gneg", align_bytes=64)
+        w2s_dealt = keep.tile([P, N], U8, name="w2s_dealt", tag="late2", align_bytes=64)
+
+        def deal_w2():
+            nc.vector.tensor_copy(
+                w2w_dealt[:].rearrange("p (t m e) -> p t m e", t=PACK, e=2), w2w[:].rearrange("p (m t e) -> p t m e", t=PACK, e=2)
+            )
+            nc.vector.tensor_copy(w2s_dealt[:].rearrange("p (t m) -> p t m", t=PACK), w2s[:].rearrange("p (m t) -> p t m", t=PACK))
 
         out_codes = sb([P, V], U32, "out_codes")
         out_scales = sb([P, V], U8, "out_scales")
@@ -239,19 +241,21 @@ def tile_picked_zwarp_abs_po_kernel(
                 out=out_codes[:, vs].bitcast(FP8X4), scales=out_scales[:, vs], in_=y_bf[:].rearrange("p v t -> p (v t)")
             )
 
-        deal_words()
-        for b in range(4):
-            open_sums(b)
-        for t, d in on_vector:
-            fused(t, d)
-        deal_scales()
+        for t in range(4):
+            for d in range(3 if t < 1 else 2):
+                fused(t, d)
+            if t in (1, 2):
+                for b in range(2):
+                    open_sums(2 * (t - 1) + b)
+        for d in (2, 3):
+            fetch(d)
         for half in range(2):
-            fetch(half)
+            weigh(2, 2 * half, 2)
         for b in range(4):
-            weigh(b)
-        for b in range(4):
+            weigh(3, b, 1)
             magnitude(b)
             turn_back(b)
+        deal_w2()
         for b in range(4):
             second(b)
         for half in range(2):

@@ -63,10 +63,10 @@ def tile_picked_zwarp_abs_po_kernel(
             nc.sync.dma_start(w1_raw[t][:], w1_rows[:, :, t * P : (t + 1) * P])
 
         ref_rows = ref.rearrange("(t p) v -> p t v", p=P)
-        ref_sb = [sb([P, 4, V // 2], F32, f"ref{h}") for h in range(2)]
+        ref_sb = [sb([P, 2, V], F32, f"ref{h}") for h in range(2)]
 
         def load_ref(h):
-            nc.sync.dma_start(ref_sb[h][:], ref_rows[:, :, h * (V // 2) : (h + 1) * (V // 2)])
+            nc.sync.dma_start(ref_sb[h][:], ref_rows[:, 2 * h : 2 * h + 2, :])
 
         xw = sb([P, T], U32, "xw")
         x_rows = x_words[0].rearrange("p n r -> p (n r)").bitcast(I32)
@@ -108,7 +108,7 @@ def tile_picked_zwarp_abs_po_kernel(
             nc.scalar.activation(gneg_by_run[:, :, 4 * k : 4 * k + 4], spread[:].rearrange("m j p -> m p j"), ACT.Copy, scale=-1.0)
 
         xg_s = [sb([P, BANK], U8, f"xg_s{h}") for h in range(2)]
-        xg_w = [sb([P, BANK], U32, f"xg_w{h}") for h in range(2)]
+        xg_w = [sb([P, BANK], U32, "xg_w0"), keep.tile([P, BANK], U32, name="xg_w1", tag="w1_bf0", align_bytes=64)]
         f = [sb([P, S], F32, f"f{t}") for t in range(4)]
 
         def first(t, h):
@@ -155,29 +155,33 @@ def tile_picked_zwarp_abs_po_kernel(
         def add_turned(b, t, block, start, stop):
             nc.tensor.matmul(e_t[b][:, t * P : (t + 1) * P], lhsT=block, rhs=ident[:], start=start, stop=stop, is_transpose=True)
 
-        def open_sums(b):
+        def open_sums():
             for t in range(4):
-                add_turned(b, t, ref_sb[b // 2][:, t, (b % 2) * P : (b % 2 + 1) * P], False, False)
+                for b in range(4):
+                    add_turned(b, t, ref_sb[t // 2][:, t % 2, b * P : (b + 1) * P], t == 0, False)
 
         W = V // 2
         rows_on_scalar = {2: list(range(1, 4)), 3: list(range(4))}
         late = {d: sb([P, len(rows_on_scalar[d]), V], F32, f"late{d}") for d in (2, 3)}
 
+        raw2 = sb([P, len(rows_on_scalar[2]), V], F32, "raw2")
+        raw = {2: raw2, 3: late[3]}
+
         def fused(t, d):
-            term = sb([P, V], F32, f"term{t}_{d}")
-            nc.vector.tensor_tensor(term[:], f[t][:].indirect(pos[d][:]), gneg[:, d, :], MULT)
+            term = raw2[:, d, :] if t == 3 else sb([P, V], F32, f"term{t}_{d}")[:]
+            nc.vector.tensor_tensor(term, f[t][:].indirect(pos[d][:]), gneg[:, d, :], MULT)
             for b in range(4):
-                add_turned(b, t, term[:, b * P : (b + 1) * P], (t, d) == (0, 0), False)
+                add_turned(b, t, term[:, b * P : (b + 1) * P], False, False)
 
         def fetch(d):
             for k, t in enumerate(rows_on_scalar[d]):
-                nc.scalar.activation(late[d][:, k, :], f[t][:].indirect(pos[d][:]), ACT.Copy)
+                nc.scalar.activation(raw[d][:, k, :], f[t][:].indirect(pos[d][:]), ACT.Copy)
 
         def weigh(d, b0, blocks):
             vs = slice(b0 * P, (b0 + blocks) * P)
             rows = late[d][:, :, vs]
             weights = gneg[:, d : d + 1, vs].to_broadcast([P, len(rows_on_scalar[d]), blocks * P])
-            nc.vector.tensor_tensor(rows, rows, weights, MULT)
+            nc.vector.tensor_tensor(rows, raw[d][:, :, vs], weights, MULT)
             for b in range(b0, b0 + blocks):
                 for k, t in enumerate(rows_on_scalar[d]):
                     add_turned(b, t, late[d][:, k, b * P : (b + 1) * P], False, d == 3 and t == 3)
@@ -241,16 +245,15 @@ def tile_picked_zwarp_abs_po_kernel(
                 out=out_codes[:, vs].bitcast(FP8X4), scales=out_scales[:, vs], in_=y_bf[:].rearrange("p v t -> p (v t)")
             )
 
-        for t in range(4):
+        open_sums()
+        for t in range(3):
             for d in range(3 if t < 1 else 2):
                 fused(t, d)
-            if t in (1, 2):
-                for b in range(2):
-                    open_sums(2 * (t - 1) + b)
         for d in (2, 3):
             fetch(d)
-        for half in range(2):
-            weigh(2, 2 * half, 2)
+        weigh(2, 0, 4)
+        for d in range(2):
+            fused(3, d)
         for b in range(4):
             weigh(3, b, 1)
             magnitude(b)

@@ -14,12 +14,20 @@ U8 = mybir.dt.uint8
 FP8X4 = mybir.dt.float8_e4m3fn_x4
 FP4X4 = mybir.dt.float4_e2m1fn_x4
 ACT = mybir.ActivationFunctionType
-MULT = mybir.AluOpType.mult
-ADD = mybir.AluOpType.add
+ALU = mybir.AluOpType
 
 P = 128
 PACK = 4
+QUAD = 32
+QUADS = P // QUAD
 BANK = 512
+PER_COLUMN = 16
+ROW_TILES = H // P
+BLOCKS = V // P
+RUN = D * V // P
+
+FETCHED = [(2, (1, 2)), (2, (3,)), (3, (0,)), (3, (1,)), (3, (2, 3))]
+LAST = len(FETCHED) - 1
 
 
 def tile_picked_zwarp_abs_po_kernel(
@@ -31,199 +39,177 @@ def tile_picked_zwarp_abs_po_kernel(
         sums = ctx.enter_context(tc.psum_pool(name="sums", bufs=1))
         ring = ctx.enter_context(tc.psum_pool(name="ring", bufs=4))
 
-        def sb(shape, dtype, name):
-            return keep.tile(shape, dtype, name=name, align_bytes=64)
+        def sb(shape, dtype, name, tag=None):
+            return keep.tile(shape, dtype, name=name, tag=tag or name, align_bytes=64)
+
+        def entries(cols):
+            return slice(cols.start // PER_COLUMN, cols.stop // PER_COLUMN)
+
+        def load_scale_rows(tile, rows):
+            for q in range(QUADS):
+                nc.sync.dma_start(tile[QUAD * q : QUAD * q + 4, :].bitcast(I32), rows[4 * q : 4 * q + 4, :].bitcast(I32))
 
         xs = sb([P, T], U8, "xs")
         nc.gpsimd.memset(xs[:].bitcast(I32), 0)
-        ones = sb([P, 32], F32, "ones")
+        ones = sb([P, QUAD], F32, "ones")
         nc.vector.memset(ones[:], 1.0)
         ident = sb([P, P], F32, "ident")
         nc.vector.memset(ident[:], 0.0)
-        column = sb([P, 32], F32, "column")
-        nc.vector.tensor_tensor_scan(column[:], ones[:], ones[:], 0.0, MULT, ADD)
+        column = sb([P, QUAD], F32, "column")
+        nc.vector.tensor_tensor_scan(column[:], ones[:], ones[:], 0.0, ALU.mult, ALU.add)
         w2s = sb([P, N], U8, "w2s")
         nc.vector.memset(w2s[:].bitcast(I32), 0)
-        row = sb([P, 32], F32, "row")
+        row = sb([P, QUAD], F32, "row")
         nc.vector.transpose(row[:], column[:])
-        for q in range(4):
-            part = slice(32 * q, 32 * (q + 1))
-            nc.vector.tensor_tensor(ident[part, part], column[part, :], row[part, :], mybir.AluOpType.is_equal)
+        for q in range(QUADS):
+            part = slice(QUAD * q, QUAD * (q + 1))
+            nc.vector.tensor_tensor(ident[part, part], column[part, :], row[part, :], ALU.is_equal)
 
-        picks = keep.tile([P, S // 16], U16, name="picks")
+        picks = keep.tile([P, S // PER_COLUMN], U16, name="picks")
         nc.sync.dma_start(picks[:], offs)
-        gcol = sb([P, 16], F32, "gcol")
-        nc.sync.dma_start(gcol[:], gate.rearrange("d r (c j) -> (d r c) j", j=16)[0 : D * P * 32 : P + 1, :])
-        for q in range(4):
-            nc.sync.dma_start(xs[32 * q : 32 * q + 4, :].bitcast(I32), x_scales[0, 4 * q : 4 * q + 4, :].bitcast(I32))
-        w1_rows = w1.rearrange("(p j) c -> p j c", j=PACK)
-        w1_raw = [sb([P, PACK, P], F32, f"w1_raw{t}") for t in range(4)]
-
-        def load_w1(t):
-            nc.sync.dma_start(w1_raw[t][:], w1_rows[:, :, t * P : (t + 1) * P])
-
-        ref_rows = ref.rearrange("(t p) v -> p t v", p=P)
-        ref_sb = [sb([P, 2, V], F32, f"ref{h}") for h in range(2)]
-
-        def load_ref(h):
-            nc.sync.dma_start(ref_sb[h][:], ref_rows[:, 2 * h : 2 * h + 2, :])
-
+        gate_runs = sb([P, RUN], F32, "gate_runs")
+        nc.sync.dma_start(gate_runs[:], gate.rearrange("d r (c j) -> (d r c) j", j=RUN)[0 : D * P * (V // RUN) : P + 1, :])
+        load_scale_rows(xs, x_scales[0])
         xw = sb([P, T], U32, "xw")
         x_rows = x_words[0].rearrange("p n r -> p (n r)").bitcast(I32)
         for h in range(2):
             cols = slice(h * (T // 2), (h + 1) * (T // 2))
             nc.sync.dma_start(xw[:, cols].bitcast(I32), x_rows[:, cols])
-        for t in range(4):
-            load_w1(t)
-        pos = []
+        w1_rows = w1.rearrange("(p j) c -> p j c", j=PACK)
+        w1_raw = [sb([P, PACK, P], F32, f"w1_raw{t}") for t in range(ROW_TILES)]
+        for t in range(ROW_TILES):
+            nc.sync.dma_start(w1_raw[t][:], w1_rows[:, :, t * P : (t + 1) * P])
+        pos = [keep.tile([P, V // PER_COLUMN], U16, name=f"pos{d}") for d in range(D)]
         for d, src in enumerate((pos1, pos2, pos3, pos4)):
-            lst = keep.tile([P, V // 16], U16, name=f"pos{d}")
-            nc.sync.dma_start(lst[:], src)
-            pos.append(lst)
-        load_ref(0)
-        load_ref(1)
+            nc.sync.dma_start(pos[d][:], src)
+        ref_rows = ref.rearrange("(t p) v -> p t v", p=P)
+        ref_sb = [sb([P, 2, V], F32, f"ref{h}") for h in range(2)]
+        for h in range(2):
+            nc.sync.dma_start(ref_sb[h][:], ref_rows[:, 2 * h : 2 * h + 2, :])
         w2w = sb([P, 2 * N], U8, "w2w")
         nc.sync.dma_start(w2w[:].bitcast(I32), w2_words[0].bitcast(I32))
-        for q in range(4):
-            nc.sync.dma_start(w2s[32 * q : 32 * q + 4, :].bitcast(I32), w2_scales[0, 4 * q : 4 * q + 4, :].bitcast(I32))
+        load_scale_rows(w2s, w2_scales[0])
 
-        w1_codes = [sb([P, P], U32, f"w1_codes{h}") for h in range(4)]
-        w1_scales = [sb([P, P], U8, f"w1_scales{h}") for h in range(4)]
-        w1_bf = [sb([P, P, PACK], BF16, f"w1_bf{h}") for h in range(4)]
-
-        def round_w1(h):
-            nc.scalar.activation(w1_bf[h][:], w1_raw[h][:].rearrange("p j c -> p c j"), ACT.Copy)
-
-        def quantise_w1(h):
-            nc.vector.quantize_mx(
-                out=w1_codes[h][:].bitcast(FP8X4), scales=w1_scales[h][:], in_=w1_bf[h][:].rearrange("p c j -> p (c j)")
+        neg_gate = sb([P, D, V], F32, "neg_gate")
+        neg_gate_runs = neg_gate[:].rearrange("m d (c j) -> m (d c) j", j=RUN)
+        per_bank = BANK // P
+        for k in range(RUN // per_bank):
+            spread = sums.tile([P, per_bank, P], F32, name=f"spread{k}", tag=f"sum{k}")
+            for j in range(per_bank):
+                at = per_bank * k + j
+                nc.tensor.transpose(spread[:, j, :], gate_runs[:, at : at + 1].to_broadcast([P, P]), ident[:])
+            nc.scalar.activation(
+                neg_gate_runs[:, :, per_bank * k : per_bank * (k + 1)], spread[:].rearrange("m j p -> m p j"), ACT.Copy, scale=-1.0
             )
 
-        gneg = sb([P, D, V], F32, "gneg")
-        gneg_by_run = gneg[:].rearrange("m d (c j) -> m (d c) j", j=16)
-        for k in range(4):
-            spread = sums.tile([P, 4, P], F32, name=f"spread{k}", tag=f"sum{k}")
-            for j in range(4):
-                nc.tensor.transpose(spread[:, j, :], gcol[:, 4 * k + j : 4 * k + j + 1].to_broadcast([P, P]), ident[:])
-            nc.scalar.activation(gneg_by_run[:, :, 4 * k : 4 * k + 4], spread[:].rearrange("m j p -> m p j"), ACT.Copy, scale=-1.0)
+        w1_codes = [sb([P, P], U32, f"w1_codes{t}") for t in range(ROW_TILES)]
+        w1_scales = [sb([P, P], U8, f"w1_scales{t}") for t in range(ROW_TILES)]
+        w1_bf = [sb([P, P, PACK], BF16, f"w1_bf{t}") for t in range(ROW_TILES)]
+        picked_scales = [sb([P, BANK], U8, f"picked_scales{h}") for h in range(2)]
+        picked_words = [sb([P, BANK], U32, "picked_words0"), sb([P, BANK], U32, "picked_words1", tag="w1_bf0")]
+        f = [sb([P, S], F32, f"f{t}") for t in range(ROW_TILES)]
 
-        xg_s = [sb([P, BANK], U8, f"xg_s{h}") for h in range(2)]
-        xg_w = [sb([P, BANK], U32, "xg_w0"), keep.tile([P, BANK], U32, name="xg_w1", tag="w1_bf0", align_bytes=64)]
-        f = [sb([P, S], F32, f"f{t}") for t in range(4)]
+        def quantise_w1(t):
+            nc.scalar.activation(w1_bf[t][:], w1_raw[t][:].rearrange("p j c -> p c j"), ACT.Copy)
+            nc.vector.quantize_mx(
+                out=w1_codes[t][:].bitcast(FP8X4), scales=w1_scales[t][:], in_=w1_bf[t][:].rearrange("p c j -> p (c j)")
+            )
 
-        def first(t, h):
-            if t < 2:
-                acc = sums.tile([P, BANK], F32, name=f"acc{t}_{h}", tag=f"sum{2 * t + h}")
-            else:
-                acc = ring.tile([P, BANK], F32, name="acc", tag="ring")
+        def pick(into, window, h, cols):
+            whole = slice(h * BANK + cols.start, h * BANK + cols.stop)
+            nc.vector.tensor_copy(into[h][:, cols], window[:].indirect(picks[:, entries(whole)]))
+
+        def first_product(t, h, cols, acc, copy):
             nc.tensor.matmul_mx(
                 out=acc[:],
                 lhsT=w1_codes[t][:].bitcast(FP8X4),
                 lhsT_scale=w1_scales[t][:],
-                rhs=xg_w[h][:].bitcast(FP8X4),
-                rhs_scale=xg_s[h][:],
+                rhs=picked_words[h][:, cols].bitcast(FP8X4),
+                rhs_scale=picked_scales[h][:, cols],
                 start=True,
                 stop=True,
             )
-            if (t, h) == (0, 1):
-                nc.vector.tensor_copy(f[t][:, h * BANK : (h + 1) * BANK], acc[:])
-            else:
-                nc.scalar.copy(f[t][:, h * BANK : (h + 1) * BANK], acc[:])
+            copy(f[t][:, h * BANK + cols.start : h * BANK + cols.stop], acc[:])
 
+        full = slice(0, BANK)
+        pieces = [slice(0, BANK // 2), slice(BANK // 2, BANK)]
         for h in range(2):
-            nc.vector.tensor_copy(xg_s[h][:], xs[:].indirect(picks[:, 32 * h : 32 * (h + 1)]))
-        nc.vector.tensor_copy(xg_w[0][:], xw[:].indirect(picks[:, 0:32]))
-        round_w1(0)
+            pick(picked_scales, xs, h, full)
+        pick(picked_words, xw, 0, full)
         quantise_w1(0)
-        nc.vector.tensor_copy(xg_w[1][:], xw[:].indirect(picks[:, 32:64]))
-        round_w1(1)
-        quantise_w1(1)
-        first(0, 0)
-        first(0, 1)
-        round_w1(2)
-        quantise_w1(2)
-        first(1, 0)
-        first(1, 1)
-        round_w1(3)
-        quantise_w1(3)
-        for t in (2, 3):
-            first(t, 0)
-            first(t, 1)
+        for cols in pieces:
+            pick(picked_words, xw, 1, cols)
+        for t in range(1, ROW_TILES):
+            quantise_w1(t)
+        first_product(0, 0, full, sums.tile([P, BANK], F32, name="acc0_0", tag="sum0"), nc.scalar.copy)
+        for cols, copy in zip(pieces, (nc.scalar.copy, nc.vector.tensor_copy)):
+            first_product(0, 1, cols, ring.tile([P, BANK // 2], F32, name="acc_piece", tag="ring"), copy)
+        for h in range(2):
+            first_product(1, h, full, sums.tile([P, BANK], F32, name=f"acc1_{h}", tag=f"sum{2 + h}"), nc.scalar.copy)
+        for t in range(2, ROW_TILES):
+            for h in range(2):
+                first_product(t, h, full, ring.tile([P, BANK], F32, name="acc", tag="ring"), nc.scalar.copy)
 
-        e_t = [sums.tile([P, H], F32, name=f"e{b}", tag=f"sum{b}") for b in range(4)]
+        e_turned = [sums.tile([P, H], F32, name=f"e{b}", tag=f"sum{b}") for b in range(BLOCKS)]
+        raw = [sb([P, len(tiles), V], F32, f"raw{g}") for g, (d, tiles) in enumerate(FETCHED)]
+        weighed = [sb([P, len(tiles), V], F32, f"weighed{g}") for g, (d, tiles) in enumerate(FETCHED[:LAST])] + [raw[LAST]]
 
-        def add_turned(b, t, block, start, stop):
-            nc.tensor.matmul(e_t[b][:, t * P : (t + 1) * P], lhsT=block, rhs=ident[:], start=start, stop=stop, is_transpose=True)
+        def add_turned(b, t, term, start=False, stop=False):
+            block = term[:, b * P : (b + 1) * P]
+            nc.tensor.matmul(e_turned[b][:, t * P : (t + 1) * P], lhsT=block, rhs=ident[:], start=start, stop=stop, is_transpose=True)
 
-        def open_sums():
-            for t in range(4):
-                for b in range(4):
-                    add_turned(b, t, ref_sb[t // 2][:, t % 2, b * P : (b + 1) * P], t == 0, False)
+        def fused(t, d, term, blocks=range(BLOCKS)):
+            vs = slice(blocks[0] * P, (blocks[-1] + 1) * P)
+            nc.vector.tensor_tensor(term[:, vs], f[t][:].indirect(pos[d][:, entries(vs)]), neg_gate[:, d, vs], ALU.mult)
+            for b in blocks:
+                add_turned(b, t, term)
 
-        W = V // 2
-        rows_on_scalar = {2: list(range(1, 4)), 3: list(range(4))}
-        late = {d: sb([P, len(rows_on_scalar[d]), V], F32, f"late{d}") for d in (2, 3)}
+        def fetch(g):
+            d, tiles = FETCHED[g]
+            for k, t in enumerate(tiles):
+                nc.scalar.activation(raw[g][:, k, :], f[t][:].indirect(pos[d][:]), ACT.Copy)
 
-        raw2 = sb([P, len(rows_on_scalar[2]), V], F32, "raw2")
-        raw = {2: raw2, 3: late[3]}
+        def weigh(g, blocks=range(BLOCKS)):
+            d, tiles = FETCHED[g]
+            vs = slice(blocks[0] * P, (blocks[-1] + 1) * P)
+            weights = neg_gate[:, d : d + 1, vs].to_broadcast([P, len(tiles), len(blocks) * P])
+            nc.vector.tensor_tensor(weighed[g][:, :, vs], raw[g][:, :, vs], weights, ALU.mult)
+            for b in blocks:
+                for k, t in enumerate(tiles):
+                    add_turned(b, t, weighed[g][:, k, :], stop=(g == LAST and k == len(tiles) - 1))
 
-        def fused(t, d):
-            term = raw2[:, d, :] if t == 3 else sb([P, V], F32, f"term{t}_{d}")[:]
-            nc.vector.tensor_tensor(term, f[t][:].indirect(pos[d][:]), gneg[:, d, :], MULT)
-            for b in range(4):
-                add_turned(b, t, term[:, b * P : (b + 1) * P], False, False)
-
-        def fetch(d):
-            for k, t in enumerate(rows_on_scalar[d]):
-                nc.scalar.activation(raw[d][:, k, :], f[t][:].indirect(pos[d][:]), ACT.Copy)
-
-        def weigh(d, b0, blocks):
-            vs = slice(b0 * P, (b0 + blocks) * P)
-            rows = late[d][:, :, vs]
-            weights = gneg[:, d : d + 1, vs].to_broadcast([P, len(rows_on_scalar[d]), blocks * P])
-            nc.vector.tensor_tensor(rows, raw[d][:, :, vs], weights, MULT)
-            for b in range(b0, b0 + blocks):
-                for k, t in enumerate(rows_on_scalar[d]):
-                    add_turned(b, t, late[d][:, k, b * P : (b + 1) * P], False, d == 3 and t == 3)
-
-        w2w_dealt = keep.tile([P, 2 * N], U8, name="w2w_dealt", tag="gneg", align_bytes=64)
-        w2s_dealt = keep.tile([P, N], U8, name="w2s_dealt", tag="late2", align_bytes=64)
-
-        def deal_w2():
-            nc.vector.tensor_copy(
-                w2w_dealt[:].rearrange("p (t m e) -> p t m e", t=PACK, e=2), w2w[:].rearrange("p (m t e) -> p t m e", t=PACK, e=2)
-            )
-            nc.vector.tensor_copy(w2s_dealt[:].rearrange("p (t m) -> p t m", t=PACK), w2s[:].rearrange("p (m t) -> p t m", t=PACK))
-
+        z_turned = [sb([P, H], BF16, f"z_turned{b}") for b in range(BLOCKS)]
+        z = [sb([P, H], BF16, f"z{b}") for b in range(BLOCKS)]
+        y = [sb([P, PACK, P], F32, f"y{b}") for b in range(BLOCKS)]
+        w2w_dealt = sb([P, 2 * N], U8, "w2w_dealt", tag="neg_gate")
+        w2s_dealt = sb([P, N], U8, "w2s_dealt", tag="weighed0")
         out_codes = sb([P, V], U32, "out_codes")
         out_scales = sb([P, V], U8, "out_scales")
         out_rows = out_0.rearrange("(p t) v -> p t v", t=PACK)
         out_words = out_1[0].rearrange("p n r -> p (n r)").bitcast(I32)
-        z = [sb([P, H], BF16, f"z{b}") for b in range(4)]
-        y = [sb([P, PACK, P], F32, f"y{b}") for b in range(4)]
 
-        z_t = [sb([P, H], BF16, f"z_t{b}") for b in range(4)]
-
-        def magnitude(b):
+        def make_z(b):
             nc.scalar.activation(
-                z_t[b][:].rearrange("v (u q e) -> v u q e", u=2, e=2), e_t[b][:].rearrange("v (q u e) -> v u q e", u=2, e=2), ACT.Abs
+                z_turned[b][:].rearrange("v (u q e) -> v u q e", u=2, e=2),
+                e_turned[b][:].rearrange("v (q u e) -> v u q e", u=2, e=2),
+                ACT.Abs,
             )
-
-        def turn_back(b):
-            turned = ring.tile([P, 2, P], F32, name="turned", tag="ring")
+            pairs = ring.tile([P, 2, P], F32, name="pairs", tag="ring")
             for u in range(2):
-                nc.tensor.transpose(turned[:, u, :], z_t[b][:].bitcast(F32)[:, u * P : (u + 1) * P], ident[:])
-            words = z[b][:].bitcast(F32).rearrange("p (v u) -> p v u", u=2)
-            if b < 2:
-                nc.scalar.copy(words, turned[:].rearrange("p u v -> p v u"))
-            else:
-                nc.vector.tensor_copy(words, turned[:].rearrange("p u v -> p v u"))
+                nc.tensor.transpose(pairs[:, u, :], z_turned[b][:].bitcast(F32)[:, u * P : (u + 1) * P], ident[:])
+            nc.vector.tensor_copy(z[b][:].bitcast(F32).rearrange("q (v u) -> q v u", u=2), pairs[:].rearrange("q u v -> q v u"))
 
-        def second(b):
+        def deal_w2():
+            nc.vector.tensor_copy(
+                w2w_dealt[:].rearrange("p (t m c) -> p t m c", t=PACK, c=2), w2w[:].rearrange("p (m t c) -> p t m c", t=PACK, c=2)
+            )
+            nc.vector.tensor_copy(w2s_dealt[:].rearrange("p (t m) -> p t m", t=PACK), w2s[:].rearrange("p (m t) -> p t m", t=PACK))
+
+        def second_product(b):
             z_codes = sb([P, P], U32, f"z_codes{b}")
             z_scales = sb([P, P], U8, f"z_scales{b}")
             nc.vector.quantize_mx(out=z_codes[:].bitcast(FP8X4), scales=z_scales[:], in_=z[b][:])
-            acc = sums.tile([P, PACK, P], F32, name=f"acc2_{b}", tag=f"sum{b}")
+            acc = sums.tile([P, PACK, P], F32, name=f"acc_out{b}", tag=f"sum{b}")
             for t in range(PACK):
                 nc.tensor.matmul_mx(
                     out=acc[:, t, :],
@@ -237,7 +223,7 @@ def tile_picked_zwarp_abs_po_kernel(
             nc.scalar.copy(y[b][:], acc[:])
             nc.sync.dma_start(out_rows[:, :, b * P : (b + 1) * P], y[b][:])
 
-        def planes(b):
+        def quantise_out(b):
             vs = slice(b * P, (b + 1) * P)
             y_bf = sb([P, P, PACK], BF16, f"y_bf{b}")
             nc.vector.tensor_copy(y_bf[:], y[b][:].rearrange("p t v -> p v t"))
@@ -245,27 +231,36 @@ def tile_picked_zwarp_abs_po_kernel(
                 out=out_codes[:, vs].bitcast(FP8X4), scales=out_scales[:, vs], in_=y_bf[:].rearrange("p v t -> p (v t)")
             )
 
-        open_sums()
-        for t in range(3):
-            for d in range(3 if t < 1 else 2):
-                fused(t, d)
-        for d in (2, 3):
-            fetch(d)
-        weigh(2, 0, 4)
-        for d in range(2):
-            fused(3, d)
-        for b in range(4):
-            weigh(3, b, 1)
-            magnitude(b)
-            turn_back(b)
+        for t in range(ROW_TILES):
+            for b in range(BLOCKS):
+                add_turned(b, t, ref_sb[t // 2][:, t % 2, :], start=(t == 0))
+        for g in range(len(FETCHED)):
+            fetch(g)
+        for t in range(2):
+            for d in range(D):
+                if not any(d == listed and t in tiles for listed, tiles in FETCHED):
+                    fused(t, d, sb([P, V], F32, f"term{t}_{d}")[:])
+        weigh(0)
+        weigh(1)
+        fused(2, 0, raw[0][:, 0, :])
+        weigh(2)
+        fused(2, 1, raw[1][:, 0, :])
+        weigh(3)
+        halves = [range(0, BLOCKS // 2), range(BLOCKS // 2, BLOCKS)]
+        for blocks in halves:
+            fused(3, 0, raw[0][:, 1, :], blocks)
+            fused(3, 1, raw[2][:, 0, :], blocks)
+            for b in blocks:
+                weigh(LAST, range(b, b + 1))
+                make_z(b)
         deal_w2()
-        for b in range(4):
-            second(b)
-        for half in range(2):
-            planes(2 * half)
-            planes(2 * half + 1)
-            vs = slice(half * W, (half + 1) * W)
+        for b in range(BLOCKS):
+            second_product(b)
+        for blocks in halves:
+            for b in blocks:
+                quantise_out(b)
+            vs = slice(blocks[0] * P, (blocks[-1] + 1) * P)
             nc.sync.dma_start(out_words[:, vs], out_codes[:, vs].bitcast(I32))
-        for q in range(4):
-            queue = nc.sync if q < 2 else nc.scalar
-            queue.dma_start(out_2[0, 4 * q : 4 * q + 4, :].bitcast(I32), out_scales[32 * q : 32 * q + 4, :].bitcast(I32))
+        for q in range(QUADS):
+            queue = nc.sync if q < QUADS // 2 else nc.scalar
+            queue.dma_start(out_2[0, 4 * q : 4 * q + 4, :].bitcast(I32), out_scales[QUAD * q : QUAD * q + 4, :].bitcast(I32))

from contextlib import ExitStack

import concourse.mybir as mybir

K, T, S, D, V, H, N = 512, 2048, 1024, 4, 512, 512, 512
FLOPS = 2 * K * H * S + 2 * H * N * V

F32 = mybir.dt.float32
BF16 = mybir.dt.bfloat16
I32 = mybir.dt.int32
U32 = mybir.dt.uint32
U16 = mybir.dt.uint16
U8 = mybir.dt.uint8
FP8X4 = mybir.dt.float8_e4m3fn_x4
FP4X4 = mybir.dt.float4_e2m1fn_x4
ACT = mybir.ActivationFunctionType
ALU = mybir.AluOpType

P = 128
PACK = 4
QUAD = 32
QUADS = P // QUAD
BANK = 512
PER_COLUMN = 16
ROW_TILES = H // P
BLOCKS = V // P
RUN = D * V // P

FETCHED = [(2, (1, 2)), (2, (3,)), (3, (0,)), (3, (1,)), (3, (2, 3))]
LAST = len(FETCHED) - 1


def tile_picked_zwarp_abs_po_kernel(
    tc, x_words, x_scales, w1, w2_words, w2_scales, gate, ref, offs, pos1, pos2, pos3, pos4, out_0, out_1, out_2
):
    nc = tc.nc
    with ExitStack() as ctx:
        keep = ctx.enter_context(tc.tile_pool(name="keep", bufs=1))
        sums = ctx.enter_context(tc.psum_pool(name="sums", bufs=1))
        ring = ctx.enter_context(tc.psum_pool(name="ring", bufs=4))

        def sb(shape, dtype, name, tag=None):
            return keep.tile(shape, dtype, name=name, tag=tag or name, align_bytes=64)

        def entries(cols):
            return slice(cols.start // PER_COLUMN, cols.stop // PER_COLUMN)

        def load_scale_rows(tile, rows):
            for q in range(QUADS):
                nc.sync.dma_start(tile[QUAD * q : QUAD * q + 4, :].bitcast(I32), rows[4 * q : 4 * q + 4, :].bitcast(I32))

        xs = sb([P, T], U8, "xs")
        nc.gpsimd.memset(xs[:].bitcast(I32), 0)
        ones = sb([P, QUAD], F32, "ones")
        nc.vector.memset(ones[:], 1.0)
        ident = sb([P, P], F32, "ident")
        nc.vector.memset(ident[:], 0.0)
        column = sb([P, QUAD], F32, "column")
        nc.vector.tensor_tensor_scan(column[:], ones[:], ones[:], 0.0, ALU.mult, ALU.add)
        w2s = sb([P, N], U8, "w2s")
        nc.vector.memset(w2s[:].bitcast(I32), 0)
        row = sb([P, QUAD], F32, "row")
        nc.vector.transpose(row[:], column[:])
        for q in range(QUADS):
            part = slice(QUAD * q, QUAD * (q + 1))
            nc.vector.tensor_tensor(ident[part, part], column[part, :], row[part, :], ALU.is_equal)

        picks = keep.tile([P, S // PER_COLUMN], U16, name="picks")
        nc.sync.dma_start(picks[:], offs)
        gate_runs = sb([P, RUN], F32, "gate_runs")
        nc.sync.dma_start(gate_runs[:], gate.rearrange("d r (c j) -> (d r c) j", j=RUN)[0 : D * P * (V // RUN) : P + 1, :])
        load_scale_rows(xs, x_scales[0])
        xw = sb([P, T], U32, "xw")
        x_rows = x_words[0].rearrange("p n r -> p (n r)").bitcast(I32)
        for h in range(2):
            cols = slice(h * (T // 2), (h + 1) * (T // 2))
            nc.sync.dma_start(xw[:, cols].bitcast(I32), x_rows[:, cols])
        w1_rows = w1.rearrange("(p j) c -> p j c", j=PACK)
        w1_raw = [sb([P, PACK, P], F32, f"w1_raw{t}") for t in range(ROW_TILES)]
        for t in range(ROW_TILES):
            nc.sync.dma_start(w1_raw[t][:], w1_rows[:, :, t * P : (t + 1) * P])
        pos = [keep.tile([P, V // PER_COLUMN], U16, name=f"pos{d}") for d in range(D)]
        for d, src in enumerate((pos1, pos2, pos3, pos4)):
            nc.sync.dma_start(pos[d][:], src)
        ref_rows = ref.rearrange("(t p) v -> p t v", p=P)
        ref_sb = [sb([P, 2, V], F32, f"ref{h}") for h in range(2)]
        for h in range(2):
            nc.sync.dma_start(ref_sb[h][:], ref_rows[:, 2 * h : 2 * h + 2, :])
        w2w = sb([P, 2 * N], U8, "w2w")
        nc.sync.dma_start(w2w[:].bitcast(I32), w2_words[0].bitcast(I32))
        load_scale_rows(w2s, w2_scales[0])

        neg_gate = sb([P, D, V], F32, "neg_gate")
        neg_gate_runs = neg_gate[:].rearrange("m d (c j) -> m (d c) j", j=RUN)
        per_bank = BANK // P
        for k in range(RUN // per_bank):
            spread = sums.tile([P, per_bank, P], F32, name=f"spread{k}", tag=f"sum{k}")
            for j in range(per_bank):
                at = per_bank * k + j
                nc.tensor.transpose(spread[:, j, :], gate_runs[:, at : at + 1].to_broadcast([P, P]), ident[:])
            nc.scalar.activation(
                neg_gate_runs[:, :, per_bank * k : per_bank * (k + 1)], spread[:].rearrange("m j p -> m p j"), ACT.Copy, scale=-1.0
            )

        w1_codes = [sb([P, P], U32, f"w1_codes{t}") for t in range(ROW_TILES)]
        w1_scales = [sb([P, P], U8, f"w1_scales{t}") for t in range(ROW_TILES)]
        w1_bf = [sb([P, P, PACK], BF16, f"w1_bf{t}") for t in range(ROW_TILES)]
        picked_scales = [sb([P, BANK], U8, f"picked_scales{h}") for h in range(2)]
        picked_words = [sb([P, BANK], U32, "picked_words0"), sb([P, BANK], U32, "picked_words1", tag="w1_bf0")]
        f = [sb([P, S], F32, f"f{t}") for t in range(ROW_TILES)]

        def quantise_w1(t):
            nc.scalar.activation(w1_bf[t][:], w1_raw[t][:].rearrange("p j c -> p c j"), ACT.Copy)
            nc.vector.quantize_mx(
                out=w1_codes[t][:].bitcast(FP8X4), scales=w1_scales[t][:], in_=w1_bf[t][:].rearrange("p c j -> p (c j)")
            )

        def pick(into, window, h, cols):
            whole = slice(h * BANK + cols.start, h * BANK + cols.stop)
            nc.vector.tensor_copy(into[h][:, cols], window[:].indirect(picks[:, entries(whole)]))

        def first_product(t, h, cols, acc, copy):
            nc.tensor.matmul_mx(
                out=acc[:],
                lhsT=w1_codes[t][:].bitcast(FP8X4),
                lhsT_scale=w1_scales[t][:],
                rhs=picked_words[h][:, cols].bitcast(FP8X4),
                rhs_scale=picked_scales[h][:, cols],
                start=True,
                stop=True,
            )
            copy(f[t][:, h * BANK + cols.start : h * BANK + cols.stop], acc[:])

        full = slice(0, BANK)
        pieces = [slice(0, BANK // 2), slice(BANK // 2, BANK)]
        for h in range(2):
            pick(picked_scales, xs, h, full)
        pick(picked_words, xw, 0, full)
        quantise_w1(0)
        for cols in pieces:
            pick(picked_words, xw, 1, cols)
        for t in range(1, ROW_TILES):
            quantise_w1(t)
        first_product(0, 0, full, sums.tile([P, BANK], F32, name="acc0_0", tag="sum0"), nc.scalar.copy)
        for cols, copy in zip(pieces, (nc.scalar.copy, nc.vector.tensor_copy)):
            first_product(0, 1, cols, ring.tile([P, BANK // 2], F32, name="acc_piece", tag="ring"), copy)
        for h in range(2):
            first_product(1, h, full, sums.tile([P, BANK], F32, name=f"acc1_{h}", tag=f"sum{2 + h}"), nc.scalar.copy)
        for t in range(2, ROW_TILES):
            for h in range(2):
                first_product(t, h, full, ring.tile([P, BANK], F32, name="acc", tag="ring"), nc.scalar.copy)

        e_turned = [sums.tile([P, H], F32, name=f"e{b}", tag=f"sum{b}") for b in range(BLOCKS)]
        raw = [sb([P, len(tiles), V], F32, f"raw{g}") for g, (d, tiles) in enumerate(FETCHED)]
        weighed = [sb([P, len(tiles), V], F32, f"weighed{g}") for g, (d, tiles) in enumerate(FETCHED[:LAST])] + [raw[LAST]]

        def add_turned(b, t, term, start=False, stop=False):
            block = term[:, b * P : (b + 1) * P]
            nc.tensor.matmul(e_turned[b][:, t * P : (t + 1) * P], lhsT=block, rhs=ident[:], start=start, stop=stop, is_transpose=True)

        def fused(t, d, term, blocks=range(BLOCKS)):
            vs = slice(blocks[0] * P, (blocks[-1] + 1) * P)
            nc.vector.tensor_tensor(term[:, vs], f[t][:].indirect(pos[d][:, entries(vs)]), neg_gate[:, d, vs], ALU.mult)
            for b in blocks:
                add_turned(b, t, term)

        def fetch(g):
            d, tiles = FETCHED[g]
            for k, t in enumerate(tiles):
                nc.scalar.activation(raw[g][:, k, :], f[t][:].indirect(pos[d][:]), ACT.Copy)

        def weigh(g, blocks=range(BLOCKS)):
            d, tiles = FETCHED[g]
            vs = slice(blocks[0] * P, (blocks[-1] + 1) * P)
            weights = neg_gate[:, d : d + 1, vs].to_broadcast([P, len(tiles), len(blocks) * P])
            nc.vector.tensor_tensor(weighed[g][:, :, vs], raw[g][:, :, vs], weights, ALU.mult)
            for b in blocks:
                for k, t in enumerate(tiles):
                    add_turned(b, t, weighed[g][:, k, :], stop=(g == LAST and k == len(tiles) - 1))

        z_turned = [sb([P, H], BF16, f"z_turned{b}") for b in range(BLOCKS)]
        z = [sb([P, H], BF16, f"z{b}") for b in range(BLOCKS)]
        y = [sb([P, PACK, P], F32, f"y{b}") for b in range(BLOCKS)]
        w2w_dealt = sb([P, 2 * N], U8, "w2w_dealt", tag="neg_gate")
        w2s_dealt = sb([P, N], U8, "w2s_dealt", tag="weighed0")
        out_codes = sb([P, V], U32, "out_codes")
        out_scales = sb([P, V], U8, "out_scales")
        out_rows = out_0.rearrange("(p t) v -> p t v", t=PACK)
        out_words = out_1[0].rearrange("p n r -> p (n r)").bitcast(I32)

        def make_z(b):
            nc.scalar.activation(
                z_turned[b][:].rearrange("v (u q e) -> v u q e", u=2, e=2),
                e_turned[b][:].rearrange("v (q u e) -> v u q e", u=2, e=2),
                ACT.Abs,
            )
            pairs = ring.tile([P, 2, P], F32, name="pairs", tag="ring")
            for u in range(2):
                nc.tensor.transpose(pairs[:, u, :], z_turned[b][:].bitcast(F32)[:, u * P : (u + 1) * P], ident[:])
            nc.vector.tensor_copy(z[b][:].bitcast(F32).rearrange("q (v u) -> q v u", u=2), pairs[:].rearrange("q u v -> q v u"))

        def deal_w2():
            nc.vector.tensor_copy(
                w2w_dealt[:].rearrange("p (t m c) -> p t m c", t=PACK, c=2), w2w[:].rearrange("p (m t c) -> p t m c", t=PACK, c=2)
            )
            nc.vector.tensor_copy(w2s_dealt[:].rearrange("p (t m) -> p t m", t=PACK), w2s[:].rearrange("p (m t) -> p t m", t=PACK))

        def second_product(b):
            z_codes = sb([P, P], U32, f"z_codes{b}")
            z_scales = sb([P, P], U8, f"z_scales{b}")
            nc.vector.quantize_mx(out=z_codes[:].bitcast(FP8X4), scales=z_scales[:], in_=z[b][:])
            acc = sums.tile([P, PACK, P], F32, name=f"acc_out{b}", tag=f"sum{b}")
            for t in range(PACK):
                nc.tensor.matmul_mx(
                    out=acc[:, t, :],
                    lhsT=w2w_dealt[:, 2 * P * t : 2 * P * (t + 1)].bitcast(FP4X4),
                    lhsT_scale=w2s_dealt[:, P * t : P * (t + 1)],
                    rhs=z_codes[:].bitcast(FP8X4),
                    rhs_scale=z_scales[:],
                    start=True,
                    stop=True,
                )
            nc.scalar.copy(y[b][:], acc[:])
            nc.sync.dma_start(out_rows[:, :, b * P : (b + 1) * P], y[b][:])

        def quantise_out(b):
            vs = slice(b * P, (b + 1) * P)
            y_bf = sb([P, P, PACK], BF16, f"y_bf{b}")
            nc.vector.tensor_copy(y_bf[:], y[b][:].rearrange("p t v -> p v t"))
            nc.vector.quantize_mx(
                out=out_codes[:, vs].bitcast(FP8X4), scales=out_scales[:, vs], in_=y_bf[:].rearrange("p v t -> p (v t)")
            )

        for t in range(ROW_TILES):
            for b in range(BLOCKS):
                add_turned(b, t, ref_sb[t // 2][:, t % 2, :], start=(t == 0))
        for g in range(len(FETCHED)):
            fetch(g)
        for t in range(2):
            for d in range(D):
                if not any(d == listed and t in tiles for listed, tiles in FETCHED):
                    fused(t, d, sb([P, V], F32, f"term{t}_{d}")[:])
        weigh(0)
        weigh(1)
        fused(2, 0, raw[0][:, 0, :])
        weigh(2)
        fused(2, 1, raw[1][:, 0, :])
        weigh(3)
        halves = [range(0, BLOCKS // 2), range(BLOCKS // 2, BLOCKS)]
        for blocks in halves:
            fused(3, 0, raw[0][:, 1, :], blocks)
            fused(3, 1, raw[2][:, 0, :], blocks)
            for b in blocks:
                weigh(LAST, range(b, b + 1))
                make_z(b)
        deal_w2()
        for b in range(BLOCKS):
            second_product(b)
        for blocks in halves:
            for b in blocks:
                quantise_out(b)
            vs = slice(blocks[0] * P, (blocks[-1] + 1) * P)
            nc.sync.dma_start(out_words[:, vs], out_codes[:, vs].bitcast(I32))
        for q in range(QUADS):
            queue = nc.sync if q < QUADS // 2 else nc.scalar
            queue.dma_start(out_2[0, 4 * q : 4 * q + 4, :].bitcast(I32), out_scales[QUAD * q : QUAD * q + 4, :].bitcast(I32))
